import numpy as np
import ml_dtypes


def mxq(x, axis, fmt="e4m3"):
    dtype, down = {"e4m3": (ml_dtypes.float8_e4m3fn, 7), "e5m2": (ml_dtypes.float8_e5m2, 14)}[fmt]
    v = np.moveaxis(np.asarray(x, np.float32).astype(ml_dtypes.bfloat16).astype(np.float64), axis, -1)
    blocks = v.reshape(v.shape[:-1] + (-1, 32))
    amax = np.abs(blocks).max(-1, keepdims=True)
    byte = np.maximum(np.where(amax > 0, np.frexp(amax)[1] - 1 + 127, 0) - down, 1)
    scale = np.exp2(byte - 127.0)
    codes = (blocks / scale).astype(np.float32).astype(dtype).astype(np.float64)
    return np.moveaxis((codes * scale).reshape(v.shape), -1, axis)


WIDE = False


def mx_kscale(k):
    if not WIDE:
        return np.ones(k)
    levels = np.array([10, -10, 5, -5, 0])
    if k % 512:
        return np.exp2(np.random.permutation(np.resize(levels, k // 32))).repeat(32)
    a = np.empty((k // 512, 16))
    for p in range(k // 512):
        a[p, :8] = np.random.permutation(np.resize(levels, 8))
        for g in range(8):
            far = levels[np.abs(levels - a[p, g]) >= 10]
            a[p, g + 8] = far[np.random.randint(len(far))]
    return np.exp2(a.ravel()).repeat(32)


def f64(x):
    return np.asarray(x).astype(np.float64)


def striped(idx):
    return np.tile(idx.reshape(-1, 16).T, (8, 1)).astype(np.uint16)


def unstriped(offs):
    return offs[:16].T.reshape(-1).astype(np.int64)


K, T, S, N = 1024, 1024, 512, 256


def setup_inputs():
    n = np.random.standard_normal
    s = mx_kscale(K)[:, None]
    return {
        "xT": (n((K, S)) * s).astype(np.float32),
        "w": (n((K, N)) / np.sqrt(K) / s).astype(np.float32),
        "b": (0.3 * n((N, 1))).astype(np.float32),
        "gate": np.tile(np.random.uniform(0.2, 1.0, S), (N, 1)).astype(np.float32),
        "offs": striped(np.random.permutation(T)[:S]),
    }


def reference(xT, w, b, gate, offs):
    idx = unstriped(offs)
    xq = mxq(f64(xT), 0, "e4m3")
    y = mxq(f64(w), 0, "e4m3").T @ xq
    y = y + f64(b)
    out = np.zeros((N, T))
    out[:, idx] = f64(gate) * y
    return out

@@ -1,0 +1,146 @@
+from contextlib import ExitStack
+
+import concourse.mybir as mybir
+
+K, T, S, N = 1024, 1024, 512, 256
+FLOPS = 2 * K * S * N
+
+F32 = mybir.dt.float32
+BF16 = mybir.dt.bfloat16
+U32 = mybir.dt.uint32
+U16 = mybir.dt.uint16
+U8 = mybir.dt.uint8
+FP8X4 = mybir.dt.float8_e4m3fn_x4
+IDENTITY = mybir.ActivationFunctionType.Identity
+MULT = mybir.AluOpType.mult
+
+P = 128
+PACK = 4
+K_PASS = P * PACK
+PASSES = K // K_PASS
+COLS = 128
+HALVES = N // COLS
+CHUNKS = S // COLS
+LIST_COLS = COLS // 16
+
+
+def tile_picked_place_lin_bias_sub_l_kernel(tc, xT, w, b, gate, offs, out):
+    nc = tc.nc
+
+    with ExitStack() as ctx:
+        keep = ctx.enter_context(tc.tile_pool(name="keep", bufs=1))
+        psum = ctx.enter_context(tc.psum_pool(name="psum", bufs=1))
+
+        def load_rows(src, g, cols, name):
+            width = cols.stop - cols.start
+            raw = keep.tile([P, PACK, width], F32, name=name)
+            rows = src[g * K_PASS : (g + 1) * K_PASS, cols]
+            nc.sync.dma_start(out=raw[:], in_=rows.rearrange("(p t) c -> p t c", t=PACK))
+            return raw
+
+        def load_gate(cols, name):
+            width = cols.stop - cols.start
+            tile = keep.tile([P, HALVES, width], F32, name=name)
+            nc.sync.dma_start(out=tile[:], in_=gate[:, cols].rearrange("(h p) c -> p h c", p=P))
+            return tile
+
+        def interleave(copy, grouped, raw):
+            copy(
+                out=grouped.rearrange("p (c i) t -> p c t i", i=4),
+                in_=raw.rearrange("p t (c i) -> p c t i", i=4),
+            )
+
+        def quantize(grouped, width, name):
+            codes = keep.tile([P, width], U32, name=name + "_codes", align_bytes=64)
+            scales = keep.tile([P, width], U8, name=name + "_scales", align_bytes=64)
+            nc.vector.quantize_mx(out=codes[:].bitcast(FP8X4), scales=scales[:], in_=grouped)
+            return codes, scales
+
+        def block(i):
+            return slice(i * COLS, (i + 1) * COLS)
+
+        on_vector, on_scalar = nc.vector.tensor_copy, nc.scalar.copy
+
+        bias = keep.tile([P, HALVES], F32)
+        with nc.allow_non_contiguous_dma(reason="one bias value a partition"):
+            nc.scalar.dma_start(out=bias[:], in_=b.rearrange("(h p) o -> p (h o)", p=P))
+
+        w_raw, x_raw, gates = {}, {}, {}
+        for g in range(PASSES):
+            w_raw[g] = load_rows(w, g, slice(0, N), f"w_raw{g}")
+            x_raw[0, g] = load_rows(xT, g, block(0), f"x_raw0{g}")
+        offsets = keep.tile([P, S // 16], U16)
+        nc.sync.dma_start(offsets[:], offs)
+        first = load_gate(block(0), "gate0")
+        for g in range(PASSES):
+            x_raw[1, g] = load_rows(xT, g, block(1), f"x_raw1{g}")
+        second = load_gate(block(1), "gate1")
+        for c in (2, 3):
+            for g in range(PASSES):
+                x_raw[c, g] = load_rows(xT, g, block(c), f"x_raw{c}{g}")
+        rest = load_gate(slice(2 * COLS, S), "gate23")
+        for h in range(HALVES):
+            gates[h, 0] = first[:, h, :]
+            gates[h, 1] = second[:, h, :]
+            gates[h, 2] = rest[:, h, block(0)]
+            gates[h, 3] = rest[:, h, block(1)]
+
+        warm = keep.tile([P, 2], F32)
+        nc.vector.memset(warm[:, 0:1], 0.0)
+        nc.scalar.activation(out=warm[:, 1:2], in_=warm[:, 0:1], func=IDENTITY)
+
+        windows = [keep.tile([P, T], F32, name=f"window{h}") for h in range(HALVES)]
+        for window in windows:
+            nc.vector.memset(window[:], 0.0)
+
+        w_mx, x_mx = {}, {}
+        for g in range(PASSES):
+            w_grouped = [keep.tile([P, COLS, PACK], BF16, name=f"w_grouped{g}{h}", align_bytes=64) for h in range(HALVES)]
+            x_grouped = keep.tile([P, COLS, PACK], BF16, name=f"x_grouped0{g}", align_bytes=64)
+            interleave(on_vector, w_grouped[0][:], w_raw[g][:, :, block(0)])
+            interleave(on_scalar, w_grouped[1][:], w_raw[g][:, :, block(1)])
+            codes, scales = quantize(w_grouped[0][:].rearrange("p c t -> p (c t)"), COLS, f"w{g}0")
+            w_mx[0, g] = (codes[:], scales[:])
+            interleave(on_vector, x_grouped[:], x_raw[0, g][:])
+            codes, scales = quantize(w_grouped[1][:].rearrange("p c t -> p (c t)"), COLS, f"w{g}1")
+            w_mx[1, g] = (codes[:], scales[:])
+            codes, scales = quantize(x_grouped[:].rearrange("p c t -> p (c t)"), COLS, f"x0{g}")
+            x_mx[0, g] = (codes[:], scales[:])
+
+        def prepare(c):
+            grouped = keep.tile([P, PASSES, COLS, PACK], BF16, name=f"x_grouped{c}", align_bytes=64)
+            for g in range(PASSES):
+                interleave(on_scalar, grouped[:, g, :, :], x_raw[c, g][:])
+            codes, scales = quantize(grouped[:].rearrange("p g c t -> p (g c t)"), PASSES * COLS, f"x{c}")
+            for g in range(PASSES):
+                x_mx[c, g] = (codes[:, block(g)], scales[:, block(g)])
+
+        def multiply(h, c):
+            acc = psum.tile([P, COLS], F32, name=f"acc{h}{c}")
+            for g in range(PASSES):
+                nc.tensor.matmul_mx(
+                    out=acc[:],
+                    lhsT=w_mx[h, g][0].bitcast(FP8X4),
+                    lhsT_scale=w_mx[h, g][1],
+                    rhs=x_mx[c, g][0].bitcast(FP8X4),
+                    rhs_scale=x_mx[c, g][1],
+                    start=(g == 0),
+                    stop=(g == PASSES - 1),
+                )
+            y = keep.tile([P, COLS], F32, name=f"y{h}{c}")
+            nc.scalar.activation(out=y[:], in_=acc[:], func=IDENTITY, bias=bias[:, h : h + 1])
+            return y
+
+        def scatter(h, c, y):
+            entries = offsets[:, c * LIST_COLS : (c + 1) * LIST_COLS]
+            nc.vector.tensor_tensor(windows[h][:].indirect(entries), y[:], gates[h, c], MULT)
+
+        for c in range(CHUNKS):
+            ys = [multiply(h, c) for h in range(HALVES)]
+            scatter(0, c, ys[0])
+            if c + 1 < CHUNKS:
+                prepare(c + 1)
+            else:
+                nc.sync.dma_start(out=out[block(0), :], in_=windows[0][:])
+            scatter(1, c, ys[1])
+        nc.sync.dma_start(out=out[block(1), :], in_=windows[1][:])

@@ -38,11 +38,11 @@ def tile_picked_place_lin_bias_sub_l_kernel(tc, xT, w, b, gate, offs, out):
             nc.sync.dma_start(out=raw[:], in_=rows.rearrange("(p t) c -> p t c", t=PACK))
             return raw
 
-        def load_gate(cols, name):
-            width = cols.stop - cols.start
-            tile = keep.tile([P, HALVES, width], F32, name=name)
-            nc.sync.dma_start(out=tile[:], in_=gate[:, cols].rearrange("(h p) c -> p h c", p=P))
-            return tile
+        def load_gate(h, first, last):
+            tile = keep.tile([P, (last - first) * COLS], F32, name=f"gate{h}{first}")
+            nc.sync.dma_start(out=tile[:], in_=gate[block(h), first * COLS : last * COLS])
+            for c in range(first, last):
+                gates[h, c] = tile[:, block(c - first)]
 
         def interleave(copy, grouped, raw):
             copy(
@@ -66,24 +66,29 @@ def tile_picked_place_lin_bias_sub_l_kernel(tc, xT, w, b, gate, offs, out):
             nc.scalar.dma_start(out=bias[:], in_=b.rearrange("(h p) o -> p (h o)", p=P))
 
         w_raw, x_raw, gates = {}, {}, {}
+
+        def load_w(h, g):
+            w_raw[h, g] = load_rows(w, g, block(h), f"w_raw{h}{g}")
+
+        def load_x(c, g):
+            x_raw[c, g] = load_rows(xT, g, block(c), f"x_raw{c}{g}")
+
         for g in range(PASSES):
-            w_raw[g] = load_rows(w, g, slice(0, N), f"w_raw{g}")
-            x_raw[0, g] = load_rows(xT, g, block(0), f"x_raw0{g}")
+            load_w(0, g)
+            load_x(0, g)
+        for g in range(PASSES):
+            load_w(1, g)
         offsets = keep.tile([P, S // 16], U16)
         nc.sync.dma_start(offsets[:], offs)
-        first = load_gate(block(0), "gate0")
-        for g in range(PASSES):
-            x_raw[1, g] = load_rows(xT, g, block(1), f"x_raw1{g}")
-        second = load_gate(block(1), "gate1")
-        for c in (2, 3):
-            for g in range(PASSES):
-                x_raw[c, g] = load_rows(xT, g, block(c), f"x_raw{c}{g}")
-        rest = load_gate(slice(2 * COLS, S), "gate23")
-        for h in range(HALVES):
-            gates[h, 0] = first[:, h, :]
-            gates[h, 1] = second[:, h, :]
-            gates[h, 2] = rest[:, h, block(0)]
-            gates[h, 3] = rest[:, h, block(1)]
+        load_gate(0, 0, 2)
+        load_x(1, 0)
+        for c in range(1, CHUNKS - 1):
+            load_x(c, 1)
+            load_x(c + 1, 0)
+            load_gate(1, c - 1, c)
+        load_x(3, 1)
+        load_gate(0, 2, 4)
+        load_gate(1, 2, 4)
 
         warm = keep.tile([P, 2], F32)
         nc.vector.memset(warm[:, 0:1], 0.0)
@@ -93,33 +98,22 @@ def tile_picked_place_lin_bias_sub_l_kernel(tc, xT, w, b, gate, offs, out):
         for window in windows:
             nc.vector.memset(window[:], 0.0)
 
-        w_mx, x_mx = {}, {}
-        for g in range(PASSES):
-            w_grouped = [keep.tile([P, COLS, PACK], BF16, name=f"w_grouped{g}{h}", align_bytes=64) for h in range(HALVES)]
-            x_grouped = keep.tile([P, COLS, PACK], BF16, name=f"x_grouped0{g}", align_bytes=64)
-            interleave(on_vector, w_grouped[0][:], w_raw[g][:, :, block(0)])
-            interleave(on_scalar, w_grouped[1][:], w_raw[g][:, :, block(1)])
-            codes, scales = quantize(w_grouped[0][:].rearrange("p c t -> p (c t)"), COLS, f"w{g}0")
-            w_mx[0, g] = (codes[:], scales[:])
-            interleave(on_vector, x_grouped[:], x_raw[0, g][:])
-            codes, scales = quantize(w_grouped[1][:].rearrange("p c t -> p (c t)"), COLS, f"w{g}1")
-            w_mx[1, g] = (codes[:], scales[:])
-            codes, scales = quantize(x_grouped[:].rearrange("p c t -> p (c t)"), COLS, f"x0{g}")
-            x_mx[0, g] = (codes[:], scales[:])
+        w_mx, x_mx, acc = {}, {}, {}
 
-        def prepare(c):
-            grouped = keep.tile([P, PASSES, COLS, PACK], BF16, name=f"x_grouped{c}", align_bytes=64)
-            for g in range(PASSES):
-                interleave(on_scalar, grouped[:, g, :, :], x_raw[c, g][:])
-            codes, scales = quantize(grouped[:].rearrange("p g c t -> p (g c t)"), PASSES * COLS, f"x{c}")
-            for g in range(PASSES):
-                x_mx[c, g] = (codes[:, block(g)], scales[:, block(g)])
+        def cast_pass(copy, raw, name):
+            grouped = keep.tile([P, COLS, PACK], BF16, name=name + "_grouped", align_bytes=64)
+            interleave(copy, grouped[:], raw)
+            return grouped
+
+        def quantize_pass(grouped, name):
+            codes, scales = quantize(grouped[:].rearrange("p c t -> p (c t)"), COLS, name)
+            return codes[:], scales[:]
 
         def multiply(h, c):
-            acc = psum.tile([P, COLS], F32, name=f"acc{h}{c}")
+            acc[h, c] = psum.tile([P, COLS], F32, name=f"acc{h}{c}")
             for g in range(PASSES):
                 nc.tensor.matmul_mx(
-                    out=acc[:],
+                    out=acc[h, c][:],
                     lhsT=w_mx[h, g][0].bitcast(FP8X4),
                     lhsT_scale=w_mx[h, g][1],
                     rhs=x_mx[c, g][0].bitcast(FP8X4),
@@ -127,20 +121,36 @@ def tile_picked_place_lin_bias_sub_l_kernel(tc, xT, w, b, gate, offs, out):
                     start=(g == 0),
                     stop=(g == PASSES - 1),
                 )
-            y = keep.tile([P, COLS], F32, name=f"y{h}{c}")
-            nc.scalar.activation(out=y[:], in_=acc[:], func=IDENTITY, bias=bias[:, h : h + 1])
-            return y
 
-        def scatter(h, c, y):
+        def put_back(h, c, y=None):
+            if y is None:
+                y = keep.tile([P, COLS], F32, name=f"y{h}{c}")[:]
+            nc.scalar.activation(out=y, in_=acc[h, c][:], func=IDENTITY, bias=bias[:, h : h + 1])
             entries = offsets[:, c * LIST_COLS : (c + 1) * LIST_COLS]
-            nc.vector.tensor_tensor(windows[h][:].indirect(entries), y[:], gates[h, c], MULT)
+            nc.vector.tensor_tensor(windows[h][:].indirect(entries), y, gates[h, c], MULT)
 
-        for c in range(CHUNKS):
-            ys = [multiply(h, c) for h in range(HALVES)]
-            scatter(0, c, ys[0])
+        def cast_x(copy, c, g):
+            x_mx[c, g] = quantize_pass(cast_pass(copy, x_raw[c, g][:], f"x{c}{g}"), f"x{c}{g}")
+
+        for g in range(PASSES):
+            w_mx[0, g] = quantize_pass(cast_pass(on_scalar, w_raw[0, g][:], f"w0{g}"), f"w0{g}")
+            cast_x(on_vector, 0, g)
+        multiply(0, 0)
+        w10 = cast_pass(on_scalar, w_raw[1, 0][:], "w10")
+        w11 = cast_pass(on_vector, w_raw[1, 1][:], "w11")
+        w_mx[1, 0] = quantize_pass(w10, "w10")
+        w_mx[1, 1] = quantize_pass(w11, "w11")
+        multiply(1, 0)
+        put_back(0, 0)
+        cast_x(on_scalar, 1, 0)
+        for c in range(1, CHUNKS):
+            cast_x(on_scalar, c, 1)
+            for h in range(HALVES):
+                multiply(h, c)
+            put_back(1, c - 1, x_raw[1, 0][:, 0, :] if c == 1 else None)
             if c + 1 < CHUNKS:
-                prepare(c + 1)
-            else:
-                nc.sync.dma_start(out=out[block(0), :], in_=windows[0][:])
-            scatter(1, c, ys[1])
+                cast_x(on_scalar, c + 1, 0)
+            put_back(0, c)
+        nc.sync.dma_start(out=out[block(0), :], in_=windows[0][:])
+        put_back(1, CHUNKS - 1)
         nc.sync.dma_start(out=out[block(1), :], in_=windows[1][:])

@@ -61,23 +61,27 @@ def tile_picked_place_lin_bias_sub_l_kernel(tc, xT, w, b, gate, offs, out):
 
         on_vector, on_scalar = nc.vector.tensor_copy, nc.scalar.copy
 
-        bias = keep.tile([P, HALVES], F32)
-        with nc.allow_non_contiguous_dma(reason="one bias value a partition"):
-            nc.scalar.dma_start(out=bias[:], in_=b.rearrange("(h p) o -> p (h o)", p=P))
-
         w_raw, x_raw, gates = {}, {}, {}
 
-        def load_w(h, g):
-            w_raw[h, g] = load_rows(w, g, block(h), f"w_raw{h}{g}")
+        def load_w(g):
+            w_raw[g] = load_rows(w, g, slice(0, N), f"w_raw{g}")
 
         def load_x(c, g):
             x_raw[c, g] = load_rows(xT, g, block(c), f"x_raw{c}{g}")
 
-        for g in range(PASSES):
-            load_w(0, g)
-            load_x(0, g)
-        for g in range(PASSES):
-            load_w(1, g)
+        load_w(0)
+        load_x(0, 0)
+        bias_rows = keep.tile([P, P], F32, align_bytes=64)
+        bias = keep.tile([P, P], F32, align_bytes=64)
+        nc.vector.memset(bias_rows[:], 0.0)
+        nc.sync.dma_start(
+            out=bias_rows[0:P:32, 0 : HALVES * 32].rearrange("q (h i) -> q h i", h=HALVES),
+            in_=b.rearrange("(h q i) o -> q h (i o)", h=HALVES, i=32),
+        )
+        nc.vector.transpose(bias[:], bias_rows[:])
+
+        load_w(1)
+        load_x(0, 1)
         offsets = keep.tile([P, S // 16], U16)
         nc.sync.dma_start(offsets[:], offs)
         load_gate(0, 0, 2)
@@ -125,7 +129,7 @@ def tile_picked_place_lin_bias_sub_l_kernel(tc, xT, w, b, gate, offs, out):
         def put_back(h, c, y=None):
             if y is None:
                 y = keep.tile([P, COLS], F32, name=f"y{h}{c}")[:]
-            nc.scalar.activation(out=y, in_=acc[h, c][:], func=IDENTITY, bias=bias[:, h : h + 1])
+            nc.scalar.activation(out=y, in_=acc[h, c][:], func=IDENTITY, bias=bias[:, 32 * h : 32 * h + 1])
             entries = offsets[:, c * LIST_COLS : (c + 1) * LIST_COLS]
             nc.vector.tensor_tensor(windows[h][:].indirect(entries), y, gates[h, c], MULT)
 
@@ -133,14 +137,14 @@ def tile_picked_place_lin_bias_sub_l_kernel(tc, xT, w, b, gate, offs, out):
             x_mx[c, g] = quantize_pass(cast_pass(copy, x_raw[c, g][:], f"x{c}{g}"), f"x{c}{g}")
 
         for g in range(PASSES):
-            w_mx[0, g] = quantize_pass(cast_pass(on_scalar, w_raw[0, g][:], f"w0{g}"), f"w0{g}")
-            cast_x(on_vector, 0, g)
-        multiply(0, 0)
-        w10 = cast_pass(on_scalar, w_raw[1, 0][:], "w10")
-        w11 = cast_pass(on_vector, w_raw[1, 1][:], "w11")
-        w_mx[1, 0] = quantize_pass(w10, "w10")
-        w_mx[1, 1] = quantize_pass(w11, "w11")
-        multiply(1, 0)
+            w_first = cast_pass(on_vector, w_raw[g][:, :, block(0)], f"w0{g}")
+            w_second = cast_pass(on_scalar, w_raw[g][:, :, block(1)], f"w1{g}")
+            w_mx[0, g] = quantize_pass(w_first, f"w0{g}")
+            x_first = cast_pass(on_vector, x_raw[0, g][:], f"x0{g}")
+            w_mx[1, g] = quantize_pass(w_second, f"w1{g}")
+            x_mx[0, g] = quantize_pass(x_first, f"x0{g}")
+        for h in range(HALVES):
+            multiply(h, 0)
         put_back(0, 0)
         cast_x(on_scalar, 1, 0)
         for c in range(1, CHUNKS):

@@ -22,6 +22,8 @@ COLS = 128
 HALVES = N // COLS
 CHUNKS = S // COLS
 LIST_COLS = COLS // 16
+LINE = 4
+SQUARE = 32
 
 
 def tile_picked_place_lin_bias_sub_l_kernel(tc, xT, w, b, gate, offs, out):
@@ -31,37 +33,18 @@ def tile_picked_place_lin_bias_sub_l_kernel(tc, xT, w, b, gate, offs, out):
         keep = ctx.enter_context(tc.tile_pool(name="keep", bufs=1))
         psum = ctx.enter_context(tc.psum_pool(name="psum", bufs=1))
 
-        def load_rows(src, g, cols, name):
-            width = cols.stop - cols.start
-            raw = keep.tile([P, PACK, width], F32, name=name)
-            rows = src[g * K_PASS : (g + 1) * K_PASS, cols]
-            nc.sync.dma_start(out=raw[:], in_=rows.rearrange("(p t) c -> p t c", t=PACK))
-            return raw
-
-        def load_gate(h, first, last):
-            tile = keep.tile([P, (last - first) * COLS], F32, name=f"gate{h}{first}")
-            nc.sync.dma_start(out=tile[:], in_=gate[block(h), first * COLS : last * COLS])
-            for c in range(first, last):
-                gates[h, c] = tile[:, block(c - first)]
-
-        def interleave(copy, grouped, raw):
-            copy(
-                out=grouped.rearrange("p (c i) t -> p c t i", i=4),
-                in_=raw.rearrange("p t (c i) -> p c t i", i=4),
-            )
-
-        def quantize(grouped, width, name):
-            codes = keep.tile([P, width], U32, name=name + "_codes", align_bytes=64)
-            scales = keep.tile([P, width], U8, name=name + "_scales", align_bytes=64)
-            nc.vector.quantize_mx(out=codes[:].bitcast(FP8X4), scales=scales[:], in_=grouped)
-            return codes, scales
+        on_vector, on_scalar = nc.vector.tensor_copy, nc.scalar.copy
+        w_raw, x_raw, gates = {}, {}, {}
+        w_mx, x_mx, acc = {}, {}, {}
 
         def block(i):
             return slice(i * COLS, (i + 1) * COLS)
 
-        on_vector, on_scalar = nc.vector.tensor_copy, nc.scalar.copy
-
-        w_raw, x_raw, gates = {}, {}, {}
+        def load_rows(src, g, cols, name):
+            raw = keep.tile([P, PACK, cols.stop - cols.start], F32, name=name)
+            rows = src[g * K_PASS : (g + 1) * K_PASS, cols]
+            nc.sync.dma_start(out=raw[:], in_=rows.rearrange("(p t) c -> p t c", t=PACK))
+            return raw
 
         def load_w(g):
             w_raw[g] = load_rows(w, g, slice(0, N), f"w_raw{g}")
@@ -69,49 +52,30 @@ def tile_picked_place_lin_bias_sub_l_kernel(tc, xT, w, b, gate, offs, out):
         def load_x(c, g):
             x_raw[c, g] = load_rows(xT, g, block(c), f"x_raw{c}{g}")
 
-        load_w(0)
-        load_x(0, 0)
-        bias_rows = keep.tile([P, P], F32, align_bytes=64)
-        bias = keep.tile([P, P], F32, align_bytes=64)
-        nc.vector.memset(bias_rows[:], 0.0)
-        nc.sync.dma_start(
-            out=bias_rows[0:P:32, 0 : HALVES * 32].rearrange("q (h i) -> q h i", h=HALVES),
-            in_=b.rearrange("(h q i) o -> q h (i o)", h=HALVES, i=32),
-        )
-        nc.vector.transpose(bias[:], bias_rows[:])
-
-        load_w(1)
-        load_x(0, 1)
-        offsets = keep.tile([P, S // 16], U16)
-        nc.sync.dma_start(offsets[:], offs)
-        load_gate(0, 0, 2)
-        load_x(1, 0)
-        for c in range(1, CHUNKS - 1):
-            load_x(c, 1)
-            load_x(c + 1, 0)
-            load_gate(1, c - 1, c)
-        load_x(3, 1)
-        load_gate(0, 2, 4)
-        load_gate(1, 2, 4)
-
-        warm = keep.tile([P, 2], F32)
-        nc.vector.memset(warm[:, 0:1], 0.0)
-        nc.scalar.activation(out=warm[:, 1:2], in_=warm[:, 0:1], func=IDENTITY)
-
-        windows = [keep.tile([P, T], F32, name=f"window{h}") for h in range(HALVES)]
-        for window in windows:
-            nc.vector.memset(window[:], 0.0)
-
-        w_mx, x_mx, acc = {}, {}, {}
+        def load_gate(h, first, last):
+            tile = keep.tile([P, (last - first) * COLS], F32, name=f"gate{h}{first}")
+            nc.sync.dma_start(out=tile[:], in_=gate[block(h), first * COLS : last * COLS])
+            for c in range(first, last):
+                gates[h, c] = tile[:, block(c - first)]
 
         def cast_pass(copy, raw, name):
             grouped = keep.tile([P, COLS, PACK], BF16, name=name + "_grouped", align_bytes=64)
-            interleave(copy, grouped[:], raw)
+            copy(
+                out=grouped[:].rearrange("p (c i) t -> p c t i", i=LINE),
+                in_=raw.rearrange("p t (c i) -> p c t i", i=LINE),
+            )
             return grouped
 
         def quantize_pass(grouped, name):
-            codes, scales = quantize(grouped[:].rearrange("p c t -> p (c t)"), COLS, name)
+            codes = keep.tile([P, COLS], U32, name=name + "_codes", align_bytes=64)
+            scales = keep.tile([P, COLS], U8, name=name + "_scales", align_bytes=64)
+            nc.vector.quantize_mx(
+                out=codes[:].bitcast(FP8X4), scales=scales[:], in_=grouped[:].rearrange("p c t -> p (c t)")
+            )
             return codes[:], scales[:]
+
+        def prepare_x(copy, c, g):
+            x_mx[c, g] = quantize_pass(cast_pass(copy, x_raw[c, g][:], f"x{c}{g}"), f"x{c}{g}")
 
         def multiply(h, c):
             acc[h, c] = psum.tile([P, COLS], F32, name=f"acc{h}{c}")
@@ -126,15 +90,49 @@ def tile_picked_place_lin_bias_sub_l_kernel(tc, xT, w, b, gate, offs, out):
                     stop=(g == PASSES - 1),
                 )
 
-        def put_back(h, c, y=None):
-            if y is None:
-                y = keep.tile([P, COLS], F32, name=f"y{h}{c}")[:]
-            nc.scalar.activation(out=y, in_=acc[h, c][:], func=IDENTITY, bias=bias[:, 32 * h : 32 * h + 1])
+        def put_back(h, c):
+            y = keep.tile([P, COLS], F32, name=f"y{h}{c}")
+            nc.scalar.activation(out=y[:], in_=acc[h, c][:], func=IDENTITY, bias=bias[:, SQUARE * h : SQUARE * h + 1])
             entries = offsets[:, c * LIST_COLS : (c + 1) * LIST_COLS]
-            nc.vector.tensor_tensor(windows[h][:].indirect(entries), y, gates[h, c], MULT)
+            nc.vector.tensor_tensor(windows[h][:].indirect(entries), y[:], gates[h, c], MULT)
 
-        def cast_x(copy, c, g):
-            x_mx[c, g] = quantize_pass(cast_pass(copy, x_raw[c, g][:], f"x{c}{g}"), f"x{c}{g}")
+        load_w(0)
+        load_x(0, 0)
+
+        bias_rows = keep.tile([P, P], F32, align_bytes=64)
+        bias = keep.tile([P, P], F32, align_bytes=64)
+        nc.vector.memset(bias_rows[:], 0.0)
+        nc.sync.dma_start(
+            out=bias_rows[0:P:SQUARE, 0 : HALVES * SQUARE].rearrange("q (h i) -> q h i", h=HALVES),
+            in_=b.rearrange("(h q i) o -> q h (i o)", h=HALVES, i=SQUARE),
+        )
+        nc.vector.transpose(bias[:], bias_rows[:])
+
+        load_w(1)
+        load_x(0, 1)
+        offsets = keep.tile([P, S // 16], U16)
+        nc.sync.dma_start(offsets[:], offs)
+
+        load_x(1, 0)
+        load_gate(0, 0, 1)
+        load_x(1, 1)
+        load_x(2, 0)
+        load_gate(1, 0, 1)
+        load_gate(0, 1, 2)
+        load_x(2, 1)
+        load_x(3, 0)
+        load_gate(1, 1, 2)
+        load_x(3, 1)
+        load_gate(0, 2, CHUNKS)
+        load_gate(1, 2, CHUNKS)
+
+        warm = keep.tile([P, 2], F32)
+        nc.vector.memset(warm[:, 0:1], 0.0)
+        nc.scalar.activation(out=warm[:, 1:2], in_=warm[:, 0:1], func=IDENTITY)
+
+        windows = [keep.tile([P, T], F32, name=f"window{h}") for h in range(HALVES)]
+        for window in windows:
+            nc.vector.memset(window[:], 0.0)
 
         for g in range(PASSES):
             w_first = cast_pass(on_vector, w_raw[g][:, :, block(0)], f"w0{g}")
@@ -145,15 +143,16 @@ def tile_picked_place_lin_bias_sub_l_kernel(tc, xT, w, b, gate, offs, out):
             x_mx[0, g] = quantize_pass(x_first, f"x0{g}")
         for h in range(HALVES):
             multiply(h, 0)
+        prepare_x(on_vector, 1, 0)
         put_back(0, 0)
-        cast_x(on_scalar, 1, 0)
+
         for c in range(1, CHUNKS):
-            cast_x(on_scalar, c, 1)
+            prepare_x(on_scalar, c, 1)
             for h in range(HALVES):
                 multiply(h, c)
-            put_back(1, c - 1, x_raw[1, 0][:, 0, :] if c == 1 else None)
+            put_back(1, c - 1)
             if c + 1 < CHUNKS:
-                cast_x(on_scalar, c + 1, 0)
+                prepare_x(on_scalar, c + 1, 0)
             put_back(0, c)
         nc.sync.dma_start(out=out[block(0), :], in_=windows[0][:])
         put_back(1, CHUNKS - 1)

from contextlib import ExitStack

import concourse.mybir as mybir

K, T, S, N = 1024, 1024, 512, 256
FLOPS = 2 * K * S * N

F32 = mybir.dt.float32
BF16 = mybir.dt.bfloat16
U32 = mybir.dt.uint32
U16 = mybir.dt.uint16
U8 = mybir.dt.uint8
FP8X4 = mybir.dt.float8_e4m3fn_x4
IDENTITY = mybir.ActivationFunctionType.Identity
MULT = mybir.AluOpType.mult

P = 128
PACK = 4
K_PASS = P * PACK
PASSES = K // K_PASS
COLS = 128
HALVES = N // COLS
CHUNKS = S // COLS
LIST_COLS = COLS // 16
LINE = 4
SQUARE = 32


def tile_picked_place_lin_bias_sub_l_kernel(tc, xT, w, b, gate, offs, out):
    nc = tc.nc

    with ExitStack() as ctx:
        keep = ctx.enter_context(tc.tile_pool(name="keep", bufs=1))
        psum = ctx.enter_context(tc.psum_pool(name="psum", bufs=1))

        on_vector, on_scalar = nc.vector.tensor_copy, nc.scalar.copy
        w_raw, x_raw, gates = {}, {}, {}
        w_mx, x_mx, acc = {}, {}, {}

        def block(i):
            return slice(i * COLS, (i + 1) * COLS)

        def load_rows(src, g, cols, name):
            raw = keep.tile([P, PACK, cols.stop - cols.start], F32, name=name)
            rows = src[g * K_PASS : (g + 1) * K_PASS, cols]
            nc.sync.dma_start(out=raw[:], in_=rows.rearrange("(p t) c -> p t c", t=PACK))
            return raw

        def load_w(g):
            w_raw[g] = load_rows(w, g, slice(0, N), f"w_raw{g}")

        def load_x(c, g):
            x_raw[c, g] = load_rows(xT, g, block(c), f"x_raw{c}{g}")

        def load_gate(h, first, last):
            tile = keep.tile([P, (last - first) * COLS], F32, name=f"gate{h}{first}")
            nc.sync.dma_start(out=tile[:], in_=gate[block(h), first * COLS : last * COLS])
            for c in range(first, last):
                gates[h, c] = tile[:, block(c - first)]

        def cast_pass(copy, raw, name):
            grouped = keep.tile([P, COLS, PACK], BF16, name=name + "_grouped", align_bytes=64)
            copy(
                out=grouped[:].rearrange("p (c i) t -> p c t i", i=LINE),
                in_=raw.rearrange("p t (c i) -> p c t i", i=LINE),
            )
            return grouped

        def quantize_pass(grouped, name):
            codes = keep.tile([P, COLS], U32, name=name + "_codes", align_bytes=64)
            scales = keep.tile([P, COLS], U8, name=name + "_scales", align_bytes=64)
            nc.vector.quantize_mx(
                out=codes[:].bitcast(FP8X4), scales=scales[:], in_=grouped[:].rearrange("p c t -> p (c t)")
            )
            return codes[:], scales[:]

        def prepare_x(copy, c, g):
            x_mx[c, g] = quantize_pass(cast_pass(copy, x_raw[c, g][:], f"x{c}{g}"), f"x{c}{g}")

        def multiply(h, c):
            acc[h, c] = psum.tile([P, COLS], F32, name=f"acc{h}{c}")
            for g in range(PASSES):
                nc.tensor.matmul_mx(
                    out=acc[h, c][:],
                    lhsT=w_mx[h, g][0].bitcast(FP8X4),
                    lhsT_scale=w_mx[h, g][1],
                    rhs=x_mx[c, g][0].bitcast(FP8X4),
                    rhs_scale=x_mx[c, g][1],
                    start=(g == 0),
                    stop=(g == PASSES - 1),
                )

        def put_back(h, c):
            y = keep.tile([P, COLS], F32, name=f"y{h}{c}")
            nc.scalar.activation(out=y[:], in_=acc[h, c][:], func=IDENTITY, bias=bias[:, SQUARE * h : SQUARE * h + 1])
            entries = offsets[:, c * LIST_COLS : (c + 1) * LIST_COLS]
            nc.vector.tensor_tensor(windows[h][:].indirect(entries), y[:], gates[h, c], MULT)

        load_w(0)
        load_x(0, 0)

        bias_rows = keep.tile([P, P], F32, align_bytes=64)
        bias = keep.tile([P, P], F32, align_bytes=64)
        nc.vector.memset(bias_rows[:], 0.0)
        nc.sync.dma_start(
            out=bias_rows[0:P:SQUARE, 0 : HALVES * SQUARE].rearrange("q (h i) -> q h i", h=HALVES),
            in_=b.rearrange("(h q i) o -> q h (i o)", h=HALVES, i=SQUARE),
        )
        nc.vector.transpose(bias[:], bias_rows[:])

        load_w(1)
        load_x(0, 1)
        offsets = keep.tile([P, S // 16], U16)
        nc.sync.dma_start(offsets[:], offs)

        load_x(1, 0)
        load_gate(0, 0, 1)
        load_x(1, 1)
        load_x(2, 0)
        load_gate(1, 0, 1)
        load_gate(0, 1, 2)
        load_x(2, 1)
        load_x(3, 0)
        load_gate(1, 1, 2)
        load_x(3, 1)
        load_gate(0, 2, CHUNKS)
        load_gate(1, 2, CHUNKS)

        warm = keep.tile([P, 2], F32)
        nc.vector.memset(warm[:, 0:1], 0.0)
        nc.scalar.activation(out=warm[:, 1:2], in_=warm[:, 0:1], func=IDENTITY)

        windows = [keep.tile([P, T], F32, name=f"window{h}") for h in range(HALVES)]
        for window in windows:
            nc.vector.memset(window[:], 0.0)

        for g in range(PASSES):
            w_first = cast_pass(on_vector, w_raw[g][:, :, block(0)], f"w0{g}")
            w_second = cast_pass(on_scalar, w_raw[g][:, :, block(1)], f"w1{g}")
            w_mx[0, g] = quantize_pass(w_first, f"w0{g}")
            x_first = cast_pass(on_vector, x_raw[0, g][:], f"x0{g}")
            w_mx[1, g] = quantize_pass(w_second, f"w1{g}")
            x_mx[0, g] = quantize_pass(x_first, f"x0{g}")
        for h in range(HALVES):
            multiply(h, 0)
        prepare_x(on_vector, 1, 0)
        put_back(0, 0)

        for c in range(1, CHUNKS):
            prepare_x(on_scalar, c, 1)
            for h in range(HALVES):
                multiply(h, c)
            put_back(1, c - 1)
            if c + 1 < CHUNKS:
                prepare_x(on_scalar, c + 1, 0)
            put_back(0, c)
        nc.sync.dma_start(out=out[block(0), :], in_=windows[0][:])
        put_back(1, CHUNKS - 1)
        nc.sync.dma_start(out=out[block(1), :], in_=windows[1][:])
